import numpy as np, ml_dtypes
CORES = [21,29,37,45,53,61,69,77,85]
N = 9
TK = 128
def setup_inputs(rng):
    return {"x": rng.standard_normal((N, 128, TK), dtype=np.float32).astype(ml_dtypes.bfloat16), "w1": (rng.standard_normal((N, 128, 128), dtype=np.float32) / 8).astype(ml_dtypes.bfloat16), "w2": (rng.standard_normal((N, 128, 128), dtype=np.float32) / 8).astype(ml_dtypes.bfloat16)}
def setup_inputs_big(rng):
    d = setup_inputs(rng)
    for k in ("x", "w1", "w2"): d[k] = (d[k].astype(np.float32) * 1024.0).astype(d[k].dtype)
    return d
def setup_inputs_small(rng):
    d = setup_inputs(rng)
    for k in ("x", "w1", "w2"): d[k] = (d[k].astype(np.float32) * (1 / 1024.0)).astype(d[k].dtype)
    return d
def setup_inputs_apart(rng):
    d = setup_inputs(rng)
    f = (10.0 ** rng.permutation(np.linspace(-1.5, 1.5, N))).astype(np.float32).reshape(N, 1, 1)
    for k in ("x", "w1", "w2"): d[k] = (d[k].astype(np.float32) * f).astype(d[k].dtype)
    return d
def reference(x, w1, w2):
    X, W1, W2 = x.astype(np.float64), w1.astype(np.float64), w2.astype(np.float64)
    y = np.zeros((N, 128, TK))
    for r in range(N):
        for j in range(N):
            y[r] += W2[j].T @ np.maximum(W1[j].T @ X[r], 0.0)
    return {"y": y.astype(ml_dtypes.bfloat16 if x.dtype != np.float64 else np.float64)}

@@ -1,0 +1,153 @@
+from concourse.bass import DstId, RemoteDMATransfer
+from concourse.mybir import AluOpType
+
+N = 9
+D = 128
+WB = 2 * D
+NB = 4
+
+SCRATCH = {
+    "wd": ("dram", [D, WB], "bfloat16"),
+    "wall": ("sbuf", [D, N * WB], "bfloat16"),
+    "xs": ("sbuf", [D, D], "bfloat16"),
+    "zero": ("sbuf", [D, D], "float32"),
+    "hs": ("sbuf", [D, N * D], "bfloat16"),
+    "ys": ("sbuf", [D, D], "bfloat16"),
+    "yacc": ("psum", [D, 512], "float32"),
+    "hp0": ("psum", [D, 512], "float32"),
+    "hp1": ("psum", [D, 512], "float32"),
+    "hp2": ("psum", [D, 512], "float32"),
+    "hp3": ("psum", [D, 512], "float32"),
+}
+SEMAPHORES = (["ldw", "ldx", "fed", "sent", "zs", "acc", "cp", "st"]
+              + ["arr%d" % j for j in range(N)]
+              + ["mm%d" % k for k in range(N)]
+              + ["rl%d" % k for k in range(N)])
+
+
+def _bits(mask):
+    return bin(mask).count("1")
+
+
+def _plan(T, topo, j):
+    cores = T.cores
+    home = cores[j]
+    others = [(j + d) % len(cores) for d in range(1, len(cores))]
+    direct = [r for r in others if topo.may_write(home, cores[r])]
+    cross = [r for r in others if not topo.may_write(home, cores[r])]
+    mate = [r for r in cross if topo.mates(topo.chip(home), topo.chip(cores[r]))]
+    far = [r for r in cross if r not in mate]
+    onchip = [c for c in range(topo.CHIPS * topo.CORES_PER_CHIP) if topo.chip(c) == topo.chip(home) and c != home]
+    ports = [c for c in onchip if all(topo.may_write(c, cores[r]) for r in cross)]
+    own_die = [c for c in ports if topo.die(c) == topo.die(home)]
+    other_die = [c for c in ports if topo.die(c) != topo.die(home)]
+    jobs = [(other_die[0], far[0::2]), (other_die[1], far[1::2]), (own_die[0], mate)]
+    return direct, [(h, d) for h, d in jobs if d]
+
+
+def _order(T, topo, r):
+    when = {}
+    for j in range(len(T.cores)):
+        if j == r:
+            continue
+        direct, jobs = _plan(T, topo, j)
+        if r in direct:
+            when[j] = 1.0 + direct.index(r)
+        for f, (h, dests) in enumerate(jobs):
+            if r in dests:
+                when[j] = 3.0 + 0.3 * (f + 1) + 1.0 + dests.index(r)
+    return sorted(when, key=lambda j: when[j])
+
+
+def _send(g, T, topo, src_core, dst_cores, mask, src, dst, sem):
+    ids = []
+    for c in dst_cores:
+        rid, pid, _se = topo.addr(c)
+        ids.append(DstId(rid=rid, pnc=pid))
+    g.remote_dma_fused([RemoteDMATransfer(dst_ids=ids, dma_engine_mask=mask, remote_sem=sem, srcs=[src],
+                                          dsts=[dst for _c in dst_cores], alu_op=0)], local_sem=T.sem.sent)
+    return _bits(mask)
+
+
+def _common_mask(topo, src_core, dst_cores):
+    m = topo.mask(src_core, dst_cores[0])
+    for c in dst_cores[1:]:
+        m &= topo.mask(src_core, c)
+    return m
+
+
+def _feed_mask(T, topo, j):
+    direct, jobs = _plan(T, topo, j)
+    home = T.cores[j]
+    on = _common_mask(topo, home, [h for h, _d in jobs])
+    off = _common_mask(topo, home, [T.cores[r] for r in direct])
+    return on & ~off, off
+
+
+def _helper(g, core, T, topo, j, dests):
+    feed, _off = _feed_mask(T, topo, j)
+    g.wait_ge(T.sem.fed, _bits(feed))
+    dst_cores = [T.cores[r] for r in dests]
+    left = _send(g, T, topo, core, dst_cores, _common_mask(topo, core, dst_cores), T.wd[:],
+                 T.wall[:, j * WB:(j + 1) * WB], T.sem["arr%d" % j])
+    g.wait_ge(T.sem.sent, left)
+
+
+def rank_program(g, core, T, topo):
+    rank = T.rank_of(core)
+    if rank is None:
+        for j in range(len(T.cores)):
+            for h, dests in _plan(T, topo, j)[1]:
+                if h == core:
+                    _helper(g, core, T, topo, j, dests)
+        return
+
+    own = rank * WB
+    g.sync.dma_start(T.wd[:, 0:D], T.w1[:]).then_inc(T.sem.ldw, 16)
+    g.scalar.dma_start(T.wd[:, D:WB], T.w2[:]).then_inc(T.sem.ldw, 16)
+    g.sync.dma_start(T.xs[:], T.x[:]).then_inc(T.sem.ldx, 16)
+    g.scalar.dma_start(T.wall[:, own:own + D], T.w1[:]).then_inc(T.sem.ldx, 16)
+    g.sync.dma_start(T.wall[:, own + D:own + WB], T.w2[:]).then_inc(T.sem.ldx, 16)
+
+    direct, jobs = _plan(T, topo, rank)
+    feed, off = _feed_mask(T, topo, rank)
+    g.wait_ge(T.sem.ldw, 32)
+    left = _send(g, T, topo, core, [h for h, _d in jobs], feed, T.wd[:], T.wd[:], T.sem.fed)
+    left += _send(g, T, topo, core, [T.cores[r] for r in direct], off, T.wd[:], T.wall[:, own:own + WB],
+                  T.sem["arr%d" % rank])
+
+    order = [rank] + _order(T, topo, rank)
+    banks = [T.hp0, T.hp1, T.hp2, T.hp3]
+    te, ve = g.tensor, g.vector
+
+    def second(k):
+        j = order[k]
+        te.wait_ge(T.sem["rl%d" % k], 1)
+        return te.matmul(T.yacc[:, 0:D], T.wall[:, j * WB + D:(j + 1) * WB], T.hs[:, k * D:(k + 1) * D],
+                         start=(k == 0), stop=(k == N - 1))
+
+    ve.memset(T.zero[:], 0.0).then_inc(T.sem.zs, 1)
+    ve.wait_ge(T.sem.zs, 1)
+    te.wait_ge(T.sem.ldx, 48)
+    for k, j in enumerate(order):
+        if j != rank:
+            sender = T.cores[j]
+            for h, dests in _plan(T, topo, j)[1]:
+                if rank in dests:
+                    sender = h
+            te.wait_ge(T.sem["arr%d" % j], _bits(topo.mask(sender, core)))
+        te.matmul(banks[k % NB][:, 0:D], T.wall[:, j * WB:j * WB + D], T.xs[:],
+                  start=True, stop=True).then_inc(T.sem["mm%d" % k], 1)
+        ve.wait_ge(T.sem["mm%d" % k], 1)
+        ve.tensor_tensor(T.hs[:, k * D:(k + 1) * D], banks[k % NB][:, 0:D], T.zero[:],
+                         op=AluOpType.max).then_inc(T.sem["rl%d" % k], 1)
+        if k >= 1:
+            second(k - 1)
+    second(N - 1).then_inc(T.sem.acc, 1)
+
+    ve.wait_ge(T.sem.acc, 1)
+    ve.tensor_copy(T.ys[:], T.yacc[:, 0:D]).then_inc(T.sem.cp, 1)
+    g.sync.wait_ge(T.sem.cp, 1)
+    g.sync.dma_start(T.y[:], T.ys[:]).then_inc(T.sem.st, 16)
+    g.sync.wait_ge(T.sem.st, 16)
+    g.wait_ge(T.sem.sent, left)

@@ -3,26 +3,31 @@ from concourse.mybir import AluOpType
 
 N = 9
 D = 128
+H = D // 2
 WB = 2 * D
-NB = 4
+NB = 3
+LAG = 2
 
 SCRATCH = {
     "wd": ("dram", [D, WB], "bfloat16"),
     "wall": ("sbuf", [D, N * WB], "bfloat16"),
     "xs": ("sbuf", [D, D], "bfloat16"),
-    "zero": ("sbuf", [D, D], "float32"),
+    "zero": ("sbuf", [D, H], "float32"),
     "hs": ("sbuf", [D, N * D], "bfloat16"),
     "ys": ("sbuf", [D, D], "bfloat16"),
-    "yacc": ("psum", [D, 512], "float32"),
-    "hp0": ("psum", [D, 512], "float32"),
-    "hp1": ("psum", [D, 512], "float32"),
-    "hp2": ("psum", [D, 512], "float32"),
-    "hp3": ("psum", [D, 512], "float32"),
+    "ya0": ("psum", [D, 512], "float32"),
+    "ya1": ("psum", [D, 512], "float32"),
+    "hp00": ("psum", [D, 512], "float32"),
+    "hp01": ("psum", [D, 512], "float32"),
+    "hp10": ("psum", [D, 512], "float32"),
+    "hp11": ("psum", [D, 512], "float32"),
+    "hp20": ("psum", [D, 512], "float32"),
+    "hp21": ("psum", [D, 512], "float32"),
 }
-SEMAPHORES = (["ldw", "ldx", "fed", "sent", "zs", "acc", "cp", "st"]
+SEMAPHORES = (["ldw", "ldx", "fed", "sent", "zs", "acc0", "acc1", "cp", "st"]
               + ["arr%d" % j for j in range(N)]
-              + ["mm%d" % k for k in range(N)]
-              + ["rl%d" % k for k in range(N)])
+              + ["mm%d_%d" % (k, s) for k in range(N) for s in (0, 1)]
+              + ["rl%d_%d" % (k, s) for k in range(N) for s in (0, 1)])
 
 
 def _bits(mask):
@@ -41,7 +46,9 @@ def _plan(T, topo, j):
     ports = [c for c in onchip if all(topo.may_write(c, cores[r]) for r in cross)]
     own_die = [c for c in ports if topo.die(c) == topo.die(home)]
     other_die = [c for c in ports if topo.die(c) != topo.die(home)]
-    jobs = [(other_die[0], far[0::2]), (other_die[1], far[1::2]), (own_die[0], mate)]
+    helpers = other_die + own_die
+    seq = far[:len(helpers) - 1] + mate + far[len(helpers) - 1:]
+    jobs = [(h, seq[k::len(helpers)]) for k, h in enumerate(helpers)]
     return direct, [(h, d) for h, d in jobs if d]
 
 
@@ -117,14 +124,17 @@ def rank_program(g, core, T, topo):
                   T.sem["arr%d" % rank])
 
     order = [rank] + _order(T, topo, rank)
-    banks = [T.hp0, T.hp1, T.hp2, T.hp3]
+    yacc = [T.ya0, T.ya1]
     te, ve = g.tensor, g.vector
 
     def second(k):
         j = order[k]
-        te.wait_ge(T.sem["rl%d" % k], 1)
-        return te.matmul(T.yacc[:, 0:D], T.wall[:, j * WB + D:(j + 1) * WB], T.hs[:, k * D:(k + 1) * D],
-                         start=(k == 0), stop=(k == N - 1))
+        for s in (0, 1):
+            te.wait_ge(T.sem["rl%d_%d" % (k, s)], 1)
+            mm = te.matmul(yacc[s][:, 0:H], T.wall[:, j * WB + D:(j + 1) * WB],
+                           T.hs[:, k * D + s * H:k * D + (s + 1) * H], start=(k == 0), stop=(k == N - 1))
+            if k == N - 1:
+                mm.then_inc(T.sem["acc%d" % s], 1)
 
     ve.memset(T.zero[:], 0.0).then_inc(T.sem.zs, 1)
     ve.wait_ge(T.sem.zs, 1)
@@ -136,18 +146,22 @@ def rank_program(g, core, T, topo):
                 if rank in dests:
                     sender = h
             te.wait_ge(T.sem["arr%d" % j], _bits(topo.mask(sender, core)))
-        te.matmul(banks[k % NB][:, 0:D], T.wall[:, j * WB:j * WB + D], T.xs[:],
-                  start=True, stop=True).then_inc(T.sem["mm%d" % k], 1)
-        ve.wait_ge(T.sem["mm%d" % k], 1)
-        ve.tensor_tensor(T.hs[:, k * D:(k + 1) * D], banks[k % NB][:, 0:D], T.zero[:],
-                         op=AluOpType.max).then_inc(T.sem["rl%d" % k], 1)
-        if k >= 1:
-            second(k - 1)
-    second(N - 1).then_inc(T.sem.acc, 1)
+        for s in (0, 1):
+            bank = T["hp%d%d" % (k % NB, s)]
+            te.matmul(bank[:, 0:H], T.wall[:, j * WB:j * WB + D], T.xs[:, s * H:(s + 1) * H],
+                      start=True, stop=True).then_inc(T.sem["mm%d_%d" % (k, s)], 1)
+            ve.wait_ge(T.sem["mm%d_%d" % (k, s)], 1)
+            ve.tensor_tensor(T.hs[:, k * D + s * H:k * D + (s + 1) * H], bank[:, 0:H], T.zero[:],
+                             op=AluOpType.max).then_inc(T.sem["rl%d_%d" % (k, s)], 1)
+        if k >= LAG:
+            second(k - LAG)
+    for k in range(N - LAG, N):
+        second(k)
 
-    ve.wait_ge(T.sem.acc, 1)
-    ve.tensor_copy(T.ys[:], T.yacc[:, 0:D]).then_inc(T.sem.cp, 1)
-    g.sync.wait_ge(T.sem.cp, 1)
+    for s in (0, 1):
+        ve.wait_ge(T.sem["acc%d" % s], 1)
+        ve.tensor_copy(T.ys[:, s * H:(s + 1) * H], yacc[s][:, 0:H]).then_inc(T.sem.cp, 1)
+    g.sync.wait_ge(T.sem.cp, 2)
     g.sync.dma_start(T.y[:], T.ys[:]).then_inc(T.sem.st, 16)
     g.sync.wait_ge(T.sem.st, 16)
     g.wait_ge(T.sem.sent, left)

@@ -9,7 +9,8 @@ NB = 3
 LAG = 2
 
 SCRATCH = {
-    "wd": ("dram", [D, WB], "bfloat16"),
+    "w1d": ("dram", [D, D], "bfloat16"),
+    "w2d": ("dram", [D, D], "bfloat16"),
     "wall": ("sbuf", [D, N * WB], "bfloat16"),
     "xs": ("sbuf", [D, D], "bfloat16"),
     "zero": ("sbuf", [D, H], "float32"),
@@ -26,12 +27,19 @@ SCRATCH = {
 }
 SEMAPHORES = (["ldw", "ldx", "fed", "sent", "zs", "acc0", "acc1", "cp", "st"]
               + ["arr%d" % j for j in range(N)]
+              + ["arb%d" % j for j in range(N)]
               + ["mm%d_%d" % (k, s) for k in range(N) for s in (0, 1)]
               + ["rl%d_%d" % (k, s) for k in range(N) for s in (0, 1)])
 
 
 def _bits(mask):
     return bin(mask).count("1")
+
+
+def _halves(mask):
+    bits = [b for b in range(mask.bit_length()) if mask >> b & 1]
+    lo = sum(1 << b for b in bits[:len(bits) // 2])
+    return lo, mask & ~lo
 
 
 def _plan(T, topo, j):
@@ -47,33 +55,46 @@ def _plan(T, topo, j):
     own_die = [c for c in ports if topo.die(c) == topo.die(home)]
     other_die = [c for c in ports if topo.die(c) != topo.die(home)]
     helpers = other_die + own_die
-    seq = far[:len(helpers) - 1] + mate + far[len(helpers) - 1:]
-    jobs = [(h, seq[k::len(helpers)]) for k, h in enumerate(helpers)]
-    return direct, [(h, d) for h, d in jobs if d]
+    n = len(helpers)
+    seq = far[:n - 1] + mate + far[n - 1:]
+    first = [[r] for r in seq[:n]] + [[] for _k in range(n - len(seq))]
+    second = [list(f) for f in first]
+    for i, r in enumerate(seq[n:]):
+        first[(2 * i) % n].insert(0, r)
+        second[(2 * i + 1) % n].append(r)
+    return direct, [(h, first[k], second[k]) for k, h in enumerate(helpers) if first[k] or second[k]]
 
 
-def _order(T, topo, r):
+def _when(T, topo, r):
     when = {}
     for j in range(len(T.cores)):
         if j == r:
             continue
         direct, jobs = _plan(T, topo, j)
         if r in direct:
-            when[j] = 1.0 + direct.index(r)
-        for f, (h, dests) in enumerate(jobs):
-            if r in dests:
-                when[j] = 3.0 + 0.3 * (f + 1) + 1.0 + dests.index(r)
-    return sorted(when, key=lambda j: when[j])
+            t = 1.0 + direct.index(r)
+            e = _bits(_common_mask(topo, T.cores[j], [T.cores[q] for q in direct]))
+            when[j] = [False, t, t, e, 0]
+            continue
+        when[j] = [True, 0.0, 0.0, 0, 0]
+        for f, (h, first, second) in enumerate(jobs):
+            base = 3.0 + 0.3 * (f + 1)
+            if r in first:
+                when[j][1] = base + 0.5 * (first.index(r) + 1)
+                when[j][3] = _bits(_common_mask(topo, h, [T.cores[q] for q in first]))
+            if r in second:
+                when[j][2] = base + 0.5 * (len(first) + second.index(r) + 1)
+                when[j][4] = _bits(_common_mask(topo, h, [T.cores[q] for q in second]))
+    return when
 
 
-def _send(g, T, topo, src_core, dst_cores, mask, src, dst, sem):
+def _transfer(topo, dst_cores, mask, src, dst, sem):
     ids = []
     for c in dst_cores:
         rid, pid, _se = topo.addr(c)
         ids.append(DstId(rid=rid, pnc=pid))
-    g.remote_dma_fused([RemoteDMATransfer(dst_ids=ids, dma_engine_mask=mask, remote_sem=sem, srcs=[src],
-                                          dsts=[dst for _c in dst_cores], alu_op=0)], local_sem=T.sem.sent)
-    return _bits(mask)
+    return RemoteDMATransfer(dst_ids=ids, dma_engine_mask=mask, remote_sem=sem, srcs=[src],
+                             dsts=[dst for _c in dst_cores], alu_op=0)
 
 
 def _common_mask(topo, src_core, dst_cores):
@@ -86,17 +107,22 @@ def _common_mask(topo, src_core, dst_cores):
 def _feed_mask(T, topo, j):
     direct, jobs = _plan(T, topo, j)
     home = T.cores[j]
-    on = _common_mask(topo, home, [h for h, _d in jobs])
+    on = _common_mask(topo, home, [job[0] for job in jobs])
     off = _common_mask(topo, home, [T.cores[r] for r in direct])
     return on & ~off, off
 
 
-def _helper(g, core, T, topo, j, dests):
+def _helper(g, core, T, topo, j, first, second):
     feed, _off = _feed_mask(T, topo, j)
     g.wait_ge(T.sem.fed, _bits(feed))
-    dst_cores = [T.cores[r] for r in dests]
-    left = _send(g, T, topo, core, dst_cores, _common_mask(topo, core, dst_cores), T.wd[:],
-                 T.wall[:, j * WB:(j + 1) * WB], T.sem["arr%d" % j])
+    left = 0
+    for dests, src, col, sem in ((first, T.w1d, j * WB, "arr%d" % j), (second, T.w2d, j * WB + D, "arb%d" % j)):
+        if dests:
+            dst_cores = [T.cores[r] for r in dests]
+            mask = _common_mask(topo, core, dst_cores)
+            g.remote_dma_fused([_transfer(topo, dst_cores, mask, src[:], T.wall[:, col:col + D], T.sem[sem])],
+                               local_sem=T.sem.sent)
+            left += _bits(mask)
     g.wait_ge(T.sem.sent, left)
 
 
@@ -104,59 +130,73 @@ def rank_program(g, core, T, topo):
     rank = T.rank_of(core)
     if rank is None:
         for j in range(len(T.cores)):
-            for h, dests in _plan(T, topo, j)[1]:
+            for h, first, second in _plan(T, topo, j)[1]:
                 if h == core:
-                    _helper(g, core, T, topo, j, dests)
+                    _helper(g, core, T, topo, j, first, second)
         return
 
     own = rank * WB
-    g.sync.dma_start(T.wd[:, 0:D], T.w1[:]).then_inc(T.sem.ldw, 16)
-    g.scalar.dma_start(T.wd[:, D:WB], T.w2[:]).then_inc(T.sem.ldw, 16)
-    g.sync.dma_start(T.xs[:], T.x[:]).then_inc(T.sem.ldx, 16)
+    g.sync.dma_start(T.w1d[:], T.w1[:]).then_inc(T.sem.ldw, 16)
+    g.scalar.dma_start(T.w2d[:], T.w2[:]).then_inc(T.sem.ldw, 16)
     g.scalar.dma_start(T.wall[:, own:own + D], T.w1[:]).then_inc(T.sem.ldx, 16)
     g.sync.dma_start(T.wall[:, own + D:own + WB], T.w2[:]).then_inc(T.sem.ldx, 16)
+    g.sync.dma_start(T.xs[:], T.x[:]).then_inc(T.sem.ldx, 16)
 
     direct, jobs = _plan(T, topo, rank)
     feed, off = _feed_mask(T, topo, rank)
+    lo, hi = _halves(feed)
+    fed_cores = [job[0] for job in jobs]
     g.wait_ge(T.sem.ldw, 32)
-    left = _send(g, T, topo, core, [h for h, _d in jobs], feed, T.wd[:], T.wd[:], T.sem.fed)
-    left += _send(g, T, topo, core, [T.cores[r] for r in direct], off, T.wd[:], T.wall[:, own:own + WB],
-                  T.sem["arr%d" % rank])
+    g.remote_dma_fused([_transfer(topo, fed_cores, lo, T.w1d[:], T.w1d[:], T.sem.fed),
+                        _transfer(topo, fed_cores, hi, T.w2d[:], T.w2d[:], T.sem.fed)], local_sem=T.sem.sent)
+    g.wait_ge(T.sem.ldx, 48)
+    g.remote_dma_fused([_transfer(topo, [T.cores[r] for r in direct], off, T.wall[:, own:own + WB],
+                                  T.wall[:, own:own + WB], T.sem["arr%d" % rank])], local_sem=T.sem.sent)
+    left = _bits(feed) + _bits(off)
 
-    order = [rank] + _order(T, topo, rank)
+    when = _when(T, topo, rank)
+    order = [rank] + sorted(when, key=lambda j: (when[j][0], when[j][1]))
+    fwd = [j != rank and when[j][0] for j in order]
+    ops = []
+    for k in range(N):
+        ops.append(("m", k))
+        if k >= LAG and not fwd[k - LAG]:
+            ops.append(("s", k - LAG))
+    rest = [k for k in range(N) if ("s", k) not in ops]
+    ops += [("s", k) for k in sorted(rest, key=lambda k: (fwd[k], when[order[k]][2] if fwd[k] else k))]
+    seconds = [k for o, k in ops if o == "s"]
+
     yacc = [T.ya0, T.ya1]
     te, ve = g.tensor, g.vector
-
-    def second(k):
-        j = order[k]
-        for s in (0, 1):
-            te.wait_ge(T.sem["rl%d_%d" % (k, s)], 1)
-            mm = te.matmul(yacc[s][:, 0:H], T.wall[:, j * WB + D:(j + 1) * WB],
-                           T.hs[:, k * D + s * H:k * D + (s + 1) * H], start=(k == 0), stop=(k == N - 1))
-            if k == N - 1:
-                mm.then_inc(T.sem["acc%d" % s], 1)
-
     ve.memset(T.zero[:], 0.0).then_inc(T.sem.zs, 1)
     ve.wait_ge(T.sem.zs, 1)
     te.wait_ge(T.sem.ldx, 48)
-    for k, j in enumerate(order):
-        if j != rank:
-            sender = T.cores[j]
-            for h, dests in _plan(T, topo, j)[1]:
-                if rank in dests:
-                    sender = h
-            te.wait_ge(T.sem["arr%d" % j], _bits(topo.mask(sender, core)))
-        for s in (0, 1):
-            bank = T["hp%d%d" % (k % NB, s)]
-            te.matmul(bank[:, 0:H], T.wall[:, j * WB:j * WB + D], T.xs[:, s * H:(s + 1) * H],
-                      start=True, stop=True).then_inc(T.sem["mm%d_%d" % (k, s)], 1)
-            ve.wait_ge(T.sem["mm%d_%d" % (k, s)], 1)
-            ve.tensor_tensor(T.hs[:, k * D + s * H:k * D + (s + 1) * H], bank[:, 0:H], T.zero[:],
-                             op=AluOpType.max).then_inc(T.sem["rl%d_%d" % (k, s)], 1)
-        if k >= LAG:
-            second(k - LAG)
-    for k in range(N - LAG, N):
-        second(k)
+    done = []
+    for o, k in ops:
+        j = order[k]
+        if o == "m":
+            if j != rank:
+                te.wait_ge(T.sem["arr%d" % j], when[j][3])
+            for s in (0, 1):
+                if k >= NB and k - NB not in done:
+                    te.wait_ge(T.sem["rl%d_%d" % (k - NB, s)], 1)
+                bank = T["hp%d%d" % (k % NB, s)]
+                te.matmul(bank[:, 0:H], T.wall[:, j * WB:j * WB + D], T.xs[:, s * H:(s + 1) * H],
+                          start=True, stop=True).then_inc(T.sem["mm%d_%d" % (k, s)], 1)
+                ve.wait_ge(T.sem["mm%d_%d" % (k, s)], 1)
+                ve.tensor_tensor(T.hs[:, k * D + s * H:k * D + (s + 1) * H], bank[:, 0:H], T.zero[:],
+                                 op=AluOpType.max).then_inc(T.sem["rl%d_%d" % (k, s)], 1)
+        else:
+            if fwd[k]:
+                te.wait_ge(T.sem["arb%d" % j], when[j][4])
+            for s in (0, 1):
+                te.wait_ge(T.sem["rl%d_%d" % (k, s)], 1)
+                mm = te.matmul(yacc[s][:, 0:H], T.wall[:, j * WB + D:(j + 1) * WB],
+                               T.hs[:, k * D + s * H:k * D + (s + 1) * H], start=(k == seconds[0]),
+                               stop=(k == seconds[-1]))
+                if k == seconds[-1]:
+                    mm.then_inc(T.sem["acc%d" % s], 1)
+            done.append(k)
 
     for s in (0, 1):
         ve.wait_ge(T.sem["acc%d" % s], 1)

from concourse.bass import DstId, RemoteDMATransfer
from concourse.mybir import AluOpType

N = 9
D = 128
H = D // 2
WB = 2 * D
NB = 3
LAG = 2

SCRATCH = {
    "w1d": ("dram", [D, D], "bfloat16"),
    "w2d": ("dram", [D, D], "bfloat16"),
    "wall": ("sbuf", [D, N * WB], "bfloat16"),
    "xs": ("sbuf", [D, D], "bfloat16"),
    "zero": ("sbuf", [D, H], "float32"),
    "hs": ("sbuf", [D, N * D], "bfloat16"),
    "ys": ("sbuf", [D, D], "bfloat16"),
    "ya0": ("psum", [D, 512], "float32"),
    "ya1": ("psum", [D, 512], "float32"),
    "hp00": ("psum", [D, 512], "float32"),
    "hp01": ("psum", [D, 512], "float32"),
    "hp10": ("psum", [D, 512], "float32"),
    "hp11": ("psum", [D, 512], "float32"),
    "hp20": ("psum", [D, 512], "float32"),
    "hp21": ("psum", [D, 512], "float32"),
}
SEMAPHORES = (["ldw", "ldx", "fed", "sent", "zs", "acc0", "acc1", "cp", "st"]
              + ["arr%d" % j for j in range(N)]
              + ["arb%d" % j for j in range(N)]
              + ["mm%d_%d" % (k, s) for k in range(N) for s in (0, 1)]
              + ["rl%d_%d" % (k, s) for k in range(N) for s in (0, 1)])


def _bits(mask):
    return bin(mask).count("1")


def _halves(mask):
    bits = [b for b in range(mask.bit_length()) if mask >> b & 1]
    lo = sum(1 << b for b in bits[:len(bits) // 2])
    return lo, mask & ~lo


def _plan(T, topo, j):
    cores = T.cores
    home = cores[j]
    others = [(j + d) % len(cores) for d in range(1, len(cores))]
    direct = [r for r in others if topo.may_write(home, cores[r])]
    cross = [r for r in others if not topo.may_write(home, cores[r])]
    mate = [r for r in cross if topo.mates(topo.chip(home), topo.chip(cores[r]))]
    far = [r for r in cross if r not in mate]
    onchip = [c for c in range(topo.CHIPS * topo.CORES_PER_CHIP) if topo.chip(c) == topo.chip(home) and c != home]
    ports = [c for c in onchip if all(topo.may_write(c, cores[r]) for r in cross)]
    own_die = [c for c in ports if topo.die(c) == topo.die(home)]
    other_die = [c for c in ports if topo.die(c) != topo.die(home)]
    helpers = other_die + own_die
    n = len(helpers)
    seq = far[:n - 1] + mate + far[n - 1:]
    first = [[r] for r in seq[:n]] + [[] for _k in range(n - len(seq))]
    second = [list(f) for f in first]
    for i, r in enumerate(seq[n:]):
        first[(2 * i) % n].insert(0, r)
        second[(2 * i + 1) % n].append(r)
    return direct, [(h, first[k], second[k]) for k, h in enumerate(helpers) if first[k] or second[k]]


def _when(T, topo, r):
    when = {}
    for j in range(len(T.cores)):
        if j == r:
            continue
        direct, jobs = _plan(T, topo, j)
        if r in direct:
            t = 1.0 + direct.index(r)
            e = _bits(_common_mask(topo, T.cores[j], [T.cores[q] for q in direct]))
            when[j] = [False, t, t, e, 0]
            continue
        when[j] = [True, 0.0, 0.0, 0, 0]
        for f, (h, first, second) in enumerate(jobs):
            base = 3.0 + 0.3 * (f + 1)
            if r in first:
                when[j][1] = base + 0.5 * (first.index(r) + 1)
                when[j][3] = _bits(_common_mask(topo, h, [T.cores[q] for q in first]))
            if r in second:
                when[j][2] = base + 0.5 * (len(first) + second.index(r) + 1)
                when[j][4] = _bits(_common_mask(topo, h, [T.cores[q] for q in second]))
    return when


def _transfer(topo, dst_cores, mask, src, dst, sem):
    ids = []
    for c in dst_cores:
        rid, pid, _se = topo.addr(c)
        ids.append(DstId(rid=rid, pnc=pid))
    return RemoteDMATransfer(dst_ids=ids, dma_engine_mask=mask, remote_sem=sem, srcs=[src],
                             dsts=[dst for _c in dst_cores], alu_op=0)


def _common_mask(topo, src_core, dst_cores):
    m = topo.mask(src_core, dst_cores[0])
    for c in dst_cores[1:]:
        m &= topo.mask(src_core, c)
    return m


def _feed_mask(T, topo, j):
    direct, jobs = _plan(T, topo, j)
    home = T.cores[j]
    on = _common_mask(topo, home, [job[0] for job in jobs])
    off = _common_mask(topo, home, [T.cores[r] for r in direct])
    return on & ~off, off


def _helper(g, core, T, topo, j, first, second):
    feed, _off = _feed_mask(T, topo, j)
    g.wait_ge(T.sem.fed, _bits(feed))
    left = 0
    for dests, src, col, sem in ((first, T.w1d, j * WB, "arr%d" % j), (second, T.w2d, j * WB + D, "arb%d" % j)):
        if dests:
            dst_cores = [T.cores[r] for r in dests]
            mask = _common_mask(topo, core, dst_cores)
            g.remote_dma_fused([_transfer(topo, dst_cores, mask, src[:], T.wall[:, col:col + D], T.sem[sem])],
                               local_sem=T.sem.sent)
            left += _bits(mask)
    g.wait_ge(T.sem.sent, left)


def rank_program(g, core, T, topo):
    rank = T.rank_of(core)
    if rank is None:
        for j in range(len(T.cores)):
            for h, first, second in _plan(T, topo, j)[1]:
                if h == core:
                    _helper(g, core, T, topo, j, first, second)
        return

    own = rank * WB
    g.sync.dma_start(T.w1d[:], T.w1[:]).then_inc(T.sem.ldw, 16)
    g.scalar.dma_start(T.w2d[:], T.w2[:]).then_inc(T.sem.ldw, 16)
    g.scalar.dma_start(T.wall[:, own:own + D], T.w1[:]).then_inc(T.sem.ldx, 16)
    g.sync.dma_start(T.wall[:, own + D:own + WB], T.w2[:]).then_inc(T.sem.ldx, 16)
    g.sync.dma_start(T.xs[:], T.x[:]).then_inc(T.sem.ldx, 16)

    direct, jobs = _plan(T, topo, rank)
    feed, off = _feed_mask(T, topo, rank)
    lo, hi = _halves(feed)
    fed_cores = [job[0] for job in jobs]
    g.wait_ge(T.sem.ldw, 32)
    g.remote_dma_fused([_transfer(topo, fed_cores, lo, T.w1d[:], T.w1d[:], T.sem.fed),
                        _transfer(topo, fed_cores, hi, T.w2d[:], T.w2d[:], T.sem.fed)], local_sem=T.sem.sent)
    g.wait_ge(T.sem.ldx, 48)
    g.remote_dma_fused([_transfer(topo, [T.cores[r] for r in direct], off, T.wall[:, own:own + WB],
                                  T.wall[:, own:own + WB], T.sem["arr%d" % rank])], local_sem=T.sem.sent)
    left = _bits(feed) + _bits(off)

    when = _when(T, topo, rank)
    order = [rank] + sorted(when, key=lambda j: (when[j][0], when[j][1]))
    fwd = [j != rank and when[j][0] for j in order]
    ops = []
    for k in range(N):
        ops.append(("m", k))
        if k >= LAG and not fwd[k - LAG]:
            ops.append(("s", k - LAG))
    rest = [k for k in range(N) if ("s", k) not in ops]
    ops += [("s", k) for k in sorted(rest, key=lambda k: (fwd[k], when[order[k]][2] if fwd[k] else k))]
    seconds = [k for o, k in ops if o == "s"]

    yacc = [T.ya0, T.ya1]
    te, ve = g.tensor, g.vector
    ve.memset(T.zero[:], 0.0).then_inc(T.sem.zs, 1)
    ve.wait_ge(T.sem.zs, 1)
    te.wait_ge(T.sem.ldx, 48)
    done = []
    for o, k in ops:
        j = order[k]
        if o == "m":
            if j != rank:
                te.wait_ge(T.sem["arr%d" % j], when[j][3])
            for s in (0, 1):
                if k >= NB and k - NB not in done:
                    te.wait_ge(T.sem["rl%d_%d" % (k - NB, s)], 1)
                bank = T["hp%d%d" % (k % NB, s)]
                te.matmul(bank[:, 0:H], T.wall[:, j * WB:j * WB + D], T.xs[:, s * H:(s + 1) * H],
                          start=True, stop=True).then_inc(T.sem["mm%d_%d" % (k, s)], 1)
                ve.wait_ge(T.sem["mm%d_%d" % (k, s)], 1)
                ve.tensor_tensor(T.hs[:, k * D + s * H:k * D + (s + 1) * H], bank[:, 0:H], T.zero[:],
                                 op=AluOpType.max).then_inc(T.sem["rl%d_%d" % (k, s)], 1)
        else:
            if fwd[k]:
                te.wait_ge(T.sem["arb%d" % j], when[j][4])
            for s in (0, 1):
                te.wait_ge(T.sem["rl%d_%d" % (k, s)], 1)
                mm = te.matmul(yacc[s][:, 0:H], T.wall[:, j * WB + D:(j + 1) * WB],
                               T.hs[:, k * D + s * H:k * D + (s + 1) * H], start=(k == seconds[0]),
                               stop=(k == seconds[-1]))
                if k == seconds[-1]:
                    mm.then_inc(T.sem["acc%d" % s], 1)
            done.append(k)

    for s in (0, 1):
        ve.wait_ge(T.sem["acc%d" % s], 1)
        ve.tensor_copy(T.ys[:, s * H:(s + 1) * H], yacc[s][:, 0:H]).then_inc(T.sem.cp, 1)
    g.sync.wait_ge(T.sem.cp, 2)
    g.sync.dma_start(T.y[:], T.ys[:]).then_inc(T.sem.st, 16)
    g.sync.wait_ge(T.sem.st, 16)
    g.wait_ge(T.sem.sent, left)
